import numpy as np
import ml_dtypes


def mxq(x, axis, fmt="e4m3"):
    dtype, down = {"e4m3": (ml_dtypes.float8_e4m3fn, 7), "e5m2": (ml_dtypes.float8_e5m2, 14)}[fmt]
    v = np.moveaxis(np.asarray(x, np.float32).astype(ml_dtypes.bfloat16).astype(np.float64), axis, -1)
    blocks = v.reshape(v.shape[:-1] + (-1, 32))
    amax = np.abs(blocks).max(-1, keepdims=True)
    byte = np.maximum(np.where(amax > 0, np.frexp(amax)[1] - 1 + 127, 0) - down, 1)
    scale = np.exp2(byte - 127.0)
    codes = (blocks / scale).astype(np.float32).astype(dtype).astype(np.float64)
    return np.moveaxis((codes * scale).reshape(v.shape), -1, axis)


WIDE = False


def mx_kscale(k):
    if not WIDE:
        return np.ones(k)
    levels = np.array([10, -10, 5, -5, 0])
    if k % 512:
        return np.exp2(np.random.permutation(np.resize(levels, k // 32))).repeat(32)
    a = np.empty((k // 512, 16))
    for p in range(k // 512):
        a[p, :8] = np.random.permutation(np.resize(levels, 8))
        for g in range(8):
            far = levels[np.abs(levels - a[p, g]) >= 10]
            a[p, g + 8] = far[np.random.randint(len(far))]
    return np.exp2(a.ravel()).repeat(32)


def f64(x):
    return np.asarray(x).astype(np.float64)


def striped(idx):
    return np.tile(idx.reshape(-1, 16).T, (8, 1)).astype(np.uint16)


def unstriped(offs):
    return offs[:16].T.reshape(-1).astype(np.int64)


def silu(v):
    return v / (1.0 + np.exp(-np.maximum(v, -700.0)))


K, T, E, C, H, N = 512, 1024, 2, 256, 1024, 256


def by_expert(wq, xq):
    return np.concatenate([wq[e].T @ xq[:, e * C:(e + 1) * C] for e in range(E)], axis=1)


def setup_inputs():
    n = np.random.standard_normal
    s = mx_kscale(K)[:, None]
    u = mx_kscale(H)
    return {
        "xT": (n((K, T)) * s).astype(np.float32),
        "w1": (n((E, K, H)) / np.sqrt(K) / s[None]).astype(np.float32),
        "w3": (n((E, K, H)) / np.sqrt(K) / s[None] * u[None, None, :]).astype(np.float32),
        "w2": (n((E, H, N)) / np.sqrt(H) / u[None, :, None]).astype(np.float32),
        "offs": striped(np.random.permutation(T)[:E * C]),
    }


def reference(xT, w1, w3, w2, offs):
    idx = unstriped(offs)
    xq = mxq(f64(xT)[:, idx], 0, "e4m3")
    h = silu(by_expert(mxq(f64(w1), 1, "e4m3"), xq))
    h = h * by_expert(mxq(f64(w3), 1, "e4m3"), xq)
    y = by_expert(mxq(f64(w2), 1, "e4m3"), mxq(h, 0, "e4m3"))
    out = np.zeros((N, T))
    out[:, idx] = y
    return out

@@ -1,0 +1,240 @@
+from contextlib import ExitStack
+
+import concourse.mybir as mybir
+
+K, T, E, C, H, N = 512, 1024, 2, 256, 1024, 256
+P = 128
+FLOPS = 2 * E * C * (2 * K * H + H * N)
+
+F32 = mybir.dt.float32
+BF16 = mybir.dt.bfloat16
+U32 = mybir.dt.uint32
+U16 = mybir.dt.uint16
+U8 = mybir.dt.uint8
+FP8X4 = mybir.dt.float8_e4m3fn_x4
+SILU = mybir.ActivationFunctionType.Silu
+MULT = mybir.AluOpType.mult
+
+CV_X = (168, 0)
+SHARE = {
+    ("w1", 0, 0): (36, 12), ("w3", 0, 0): (36, 12), ("w1", 0, 1): (36, 12), ("w3", 0, 1): (36, 12),
+    ("w2", 0, 0): (0, 8), ("w2", 0, 1): (0, 8),
+    ("w1", 1, 0): (36, 12), ("w3", 1, 0): (36, 12), ("w1", 1, 1): (36, 12), ("w3", 1, 1): (36, 12),
+    ("w2", 1, 0): (16, 8), ("w2", 1, 1): (16, 8),
+}
+ADD = mybir.AluOpType.add
+
+
+def split_copy(nc, dst, src, share):
+    n = dst.shape[1]
+    a = share[0]
+    b = share[0] + share[1]
+    if a > 0:
+        nc.vector.tensor_copy(out=dst[:, :a], in_=src[:, :a])
+    if b > a:
+        nc.gpsimd.tensor_scalar(out=dst[:, a:b], in0=src[:, a:b], scalar1=1.0, scalar2=0.0, op0=MULT, op1=ADD)
+    if b < n:
+        nc.scalar.copy(out=dst[:, b:], in_=src[:, b:])
+
+
+def tile_routed_moe_kernel(tc, xT, w1, w3, w2, offs, out):
+    nc = tc.nc
+    with ExitStack() as ctx:
+        lists = ctx.enter_context(tc.tile_pool(name="lists", bufs=1))
+        keep = ctx.enter_context(tc.tile_pool(name="keep", bufs=1))
+        grp_pool = ctx.enter_context(tc.tile_pool(name="grp_pool", bufs=4))
+        sa_pool = ctx.enter_context(tc.tile_pool(name="sa_pool", bufs=3))
+        hg_pool = ctx.enter_context(tc.tile_pool(name="hg_pool", bufs=2))
+        y_pool = ctx.enter_context(tc.tile_pool(name="y_pool", bufs=4))
+        psum_a = ctx.enter_context(tc.psum_pool(name="psum_a", bufs=3))
+        psum_b = ctx.enter_context(tc.psum_pool(name="psum_b", bufs=3))
+        psum_y = ctx.enter_context(tc.psum_pool(name="psum_y", bufs=2))
+
+        offs_t = lists.tile([P, E * C // 16], U16, name="offs_t")
+        nc.sync.dma_start(offs_t[:], offs)
+
+        x_rows = xT.rearrange("(p j) n -> p j n", j=4)
+        x_raw = []
+        for u in range(2):
+            t = keep.tile([P, 2, T], F32, name="x_raw%d" % u)
+            nc.sync.dma_start(t[:], x_rows[:, 2 * u:2 * u + 2, :])
+            x_raw.append(t)
+
+        steps = []
+        for e in range(E):
+            for g in range(2):
+                steps.append(("w1", e, g))
+                steps.append(("w3", e, g))
+        for e in range(E):
+            for g in range(2):
+                steps.append(("w2", e, g))
+
+        raw = {}
+        for st in steps:
+            kind, e, g = st
+            if kind == "w2":
+                t = keep.tile([P, 4, N], F32, name="raw_%s_%d_%d" % st)
+                nc.sync.dma_start(t[:], w2[e, 512 * g:512 * (g + 1), :].rearrange("(p j) n -> p j n", j=4))
+            else:
+                w = w1 if kind == "w1" else w3
+                t = keep.tile([P, 4, 512], F32, name="raw_%s_%d_%d" % st)
+                nc.sync.dma_start(t[:], w[e].rearrange("(p j) c -> p j c", j=4)[:, :, 512 * g:512 * (g + 1)])
+            raw[st] = t
+
+        win = []
+        for nt in range(2):
+            t = keep.tile([P, T], F32, name="win%d" % nt)
+            nc.vector.memset(t[:], 0.0)
+            win.append(t)
+        warm_in = keep.tile([P, 1], F32, name="warm_in")
+        warm_out = keep.tile([P, 1], F32, name="warm_out")
+        nc.vector.memset(warm_in[:], 0.0)
+        nc.scalar.activation(out=warm_out[:], in_=warm_in[:], func=SILU)
+
+        xg = keep.tile([P, 4 * E * C], BF16, name="xg", align_bytes=64)
+        xg_words = xg[:].bitcast(U32).rearrange("p (n u) -> p n u", u=2)
+        for u in range(2):
+            pair = keep.tile([P, 2 * T], BF16, name="pair%d" % u, align_bytes=64)
+            split_copy(
+                nc,
+                pair[:].rearrange("p (c i e) -> p c e i", i=4, e=2),
+                x_raw[u][:].rearrange("p e (c i) -> p c e i", i=4),
+                CV_X,
+            )
+            nc.vector.tensor_copy(out=xg_words[:, :, u], in_=pair[:].bitcast(U32).indirect(offs_t[:]))
+        xc = keep.tile([P, E * C], U32, name="xc", align_bytes=64)
+        xs = keep.tile([P, E * C], U8, name="xs", align_bytes=64)
+
+        grouped = {}
+        codes = {}
+        scales = {}
+        sa = {}
+        hg = {}
+        hcodes = {}
+        hscales = {}
+        ybank = {}
+
+        def cast(st):
+            kind, e, g = st
+            if kind == "w2":
+                t = grp_pool.tile([P, 4 * N], BF16, name="grp2", tag="grp2", align_bytes=64)
+                split_copy(
+                    nc,
+                    t[:].rearrange("p (c i j) -> p c j i", i=4, j=4),
+                    raw[st][:].rearrange("p j (c i) -> p c j i", i=4),
+                    SHARE[st],
+                )
+            else:
+                t = grp_pool.tile([P, 4 * 512], BF16, name="grp", tag="grp", align_bytes=64)
+                split_copy(
+                    nc,
+                    t[:].rearrange("p (t m j) -> p m j t", t=4, j=4),
+                    raw[st][:].rearrange("p j (m t) -> p m j t", t=4),
+                    SHARE[st],
+                )
+            grouped[st] = t
+
+        def quant(st):
+            width = grouped[st].shape[1] // 4
+            c = keep.tile([P, width], U32, name="c_%s_%d_%d" % st, align_bytes=64)
+            s = keep.tile([P, width], U8, name="s_%s_%d_%d" % st, align_bytes=64)
+            nc.vector.quantize_mx(out=c[:].bitcast(FP8X4), scales=s[:], in_=grouped[st][:])
+            codes[st] = c
+            scales[st] = s
+
+        def stage1(st, pool, half):
+            kind, e, g = st
+            bank = pool.tile([P, 4, 128], F32, name="bank_" + kind, tag="bank_" + kind)
+            cols = slice(e * C + 128 * half, e * C + 128 * (half + 1))
+            for t in range(4):
+                nc.tensor.matmul_mx(
+                    out=bank[:, t, :],
+                    lhsT=codes[st][:, 128 * t:128 * (t + 1)].bitcast(FP8X4),
+                    lhsT_scale=scales[st][:, 128 * t:128 * (t + 1)],
+                    rhs=xc[:, cols].bitcast(FP8X4),
+                    rhs_scale=xs[:, cols],
+                    start=True,
+                    stop=True,
+                )
+            return bank
+
+        def quant_h(e, g):
+            c = keep.tile([P, C], U32, name="hc_%d_%d" % (e, g), align_bytes=64)
+            s = keep.tile([P, C], U8, name="hs_%d_%d" % (e, g), align_bytes=64)
+            nc.vector.quantize_mx(out=c[:].bitcast(FP8X4), scales=s[:], in_=hg[(e, g)][:])
+            hcodes[(e, g)] = c
+            hscales[(e, g)] = s
+
+        def post(st):
+            kind, e, g = st
+            if kind == "w1":
+                for half in range(2):
+                    bank = stage1(st, psum_a, half)
+                    t = sa_pool.tile([P, 512], F32, name="sa", tag="sa")
+                    nc.scalar.activation(
+                        out=t[:].rearrange("p (n t) -> p n t", t=4),
+                        in_=bank[:].rearrange("p t n -> p n t"),
+                        func=SILU,
+                    )
+                    sa[(e, g, half)] = t
+            elif kind == "w3":
+                h = hg_pool.tile([P, 4 * C], BF16, name="hg", tag="hg", align_bytes=64)
+                hg[(e, g)] = h
+                for half in range(2):
+                    bank = stage1(st, psum_b, half)
+                    nc.vector.tensor_tensor(
+                        out=h[:, 512 * half:512 * (half + 1)].rearrange("p (n t) -> p n t", t=4),
+                        in0=sa[(e, g, half)][:].rearrange("p (n t) -> p n t", t=4),
+                        in1=bank[:].rearrange("p t n -> p n t"),
+                        op=MULT,
+                    )
+                pending.append((e, g))
+
+        def stage2():
+            for e in range(E):
+                for g in range(2):
+                    if (e, g) in done2 or (e, g) not in hcodes or ("w2", e, g) not in codes:
+                        continue
+                    if g == 1 and (e, 0) not in done2:
+                        continue
+                    done2.add((e, g))
+                    st = ("w2", e, g)
+                    for nt in range(2):
+                        if g == 0:
+                            ybank[(e, nt)] = psum_y.tile([P, C], F32, name="ybank", tag="ybank")
+                        nc.tensor.matmul_mx(
+                            out=ybank[(e, nt)][:],
+                            lhsT=codes[st][:, 128 * nt:128 * (nt + 1)].bitcast(FP8X4),
+                            lhsT_scale=scales[st][:, 128 * nt:128 * (nt + 1)],
+                            rhs=hcodes[(e, g)][:].bitcast(FP8X4),
+                            rhs_scale=hscales[(e, g)][:],
+                            start=(g == 0),
+                            stop=(g == 1),
+                        )
+                    if g == 1:
+                        for nt in range(2):
+                            y = y_pool.tile([P, C], F32, name="y", tag="y")
+                            nc.scalar.copy(out=y[:], in_=ybank[(e, nt)][:])
+                            nc.vector.tensor_copy(
+                                out=win[nt][:].indirect(offs_t[:, 16 * e:16 * (e + 1)]),
+                                in_=y[:],
+                            )
+                            if e == E - 1:
+                                nc.sync.dma_start(out[128 * nt:128 * (nt + 1), :], win[nt][:])
+
+        done2 = set()
+        pending = []
+        cast(steps[0])
+        nc.vector.quantize_mx(out=xc[:].bitcast(FP8X4), scales=xs[:], in_=xg[:])
+        for i in range(len(steps)):
+            if i + 1 < len(steps):
+                cast(steps[i + 1])
+            quant(steps[i])
+            for eg in pending:
+                quant_h(eg[0], eg[1])
+            pending.clear()
+            stage2()
+            post(steps[i])
+        for eg in pending:
+            quant_h(eg[0], eg[1])
+        stage2()

@@ -17,9 +17,9 @@ MULT = mybir.AluOpType.mult
 
 CV_X = (168, 0)
 SHARE = {
-    ("w1", 0, 0): (36, 12), ("w3", 0, 0): (36, 12), ("w1", 0, 1): (36, 12), ("w3", 0, 1): (36, 12),
+    ("w1", 0, 0): (44, 12), ("w3", 0, 0): (44, 12), ("w1", 0, 1): (44, 12), ("w3", 0, 1): (44, 12),
     ("w2", 0, 0): (0, 8), ("w2", 0, 1): (0, 8),
-    ("w1", 1, 0): (36, 12), ("w3", 1, 0): (36, 12), ("w1", 1, 1): (36, 12), ("w3", 1, 1): (36, 12),
+    ("w1", 1, 0): (44, 12), ("w3", 1, 0): (44, 12), ("w1", 1, 1): (44, 12), ("w3", 1, 1): (44, 12),
     ("w2", 1, 0): (16, 8), ("w2", 1, 1): (16, 8),
 }
 ADD = mybir.AluOpType.add

@@ -25,7 +25,9 @@ SHARE = {
 ADD = mybir.AluOpType.add
 
 
-def split_copy(nc, dst, src, share):
+def split_copy(nc, dst, src, share, scalar_dst=None, scalar_src=None):
+    scalar_dst = dst if scalar_dst is None else scalar_dst
+    scalar_src = src if scalar_src is None else scalar_src
     n = dst.shape[1]
     a = share[0]
     b = share[0] + share[1]
@@ -34,7 +36,7 @@ def split_copy(nc, dst, src, share):
     if b > a:
         nc.gpsimd.tensor_scalar(out=dst[:, a:b], in0=src[:, a:b], scalar1=1.0, scalar2=0.0, op0=MULT, op1=ADD)
     if b < n:
-        nc.scalar.copy(out=dst[:, b:], in_=src[:, b:])
+        nc.scalar.copy(out=scalar_dst[:, b:], in_=scalar_src[:, b:])
 
 
 def tile_routed_moe_kernel(tc, xT, w1, w3, w2, offs, out):
@@ -131,6 +133,8 @@ def tile_routed_moe_kernel(tc, xT, w1, w3, w2, offs, out):
                     t[:].rearrange("p (t m j) -> p m j t", t=4, j=4),
                     raw[st][:].rearrange("p j (m t) -> p m j t", t=4),
                     SHARE[st],
+                    t[:].rearrange("p (t m a b) -> p m a t b", t=4, a=2, b=2),
+                    raw[st][:].rearrange("p (a b) (m t) -> p m a t b", b=2, t=4),
                 )
             grouped[st] = t
 

@@ -18,9 +18,9 @@ MULT = mybir.AluOpType.mult
 CV_X = (168, 0)
 SHARE = {
     ("w1", 0, 0): (44, 12), ("w3", 0, 0): (44, 12), ("w1", 0, 1): (44, 12), ("w3", 0, 1): (44, 12),
-    ("w2", 0, 0): (0, 8), ("w2", 0, 1): (0, 8),
+    ("w2", 0, 0): (16, 8), ("w2", 0, 1): (64, 0),
     ("w1", 1, 0): (44, 12), ("w3", 1, 0): (44, 12), ("w1", 1, 1): (44, 12), ("w3", 1, 1): (44, 12),
-    ("w2", 1, 0): (16, 8), ("w2", 1, 1): (16, 8),
+    ("w2", 1, 0): (0, 8), ("w2", 1, 1): (16, 8),
 }
 ADD = mybir.AluOpType.add
 

@@ -18,9 +18,9 @@ MULT = mybir.AluOpType.mult
 CV_X = (168, 0)
 SHARE = {
     ("w1", 0, 0): (44, 12), ("w3", 0, 0): (44, 12), ("w1", 0, 1): (44, 12), ("w3", 0, 1): (44, 12),
-    ("w2", 0, 0): (16, 8), ("w2", 0, 1): (64, 0),
-    ("w1", 1, 0): (44, 12), ("w3", 1, 0): (44, 12), ("w1", 1, 1): (44, 12), ("w3", 1, 1): (44, 12),
-    ("w2", 1, 0): (0, 8), ("w2", 1, 1): (16, 8),
+    ("w2", 0, 0): (24, 0), ("w2", 0, 1): (64, 0),
+    ("w1", 1, 0): (44, 12), ("w3", 1, 0): (44, 12), ("w1", 1, 1): (44, 12), ("w3", 1, 1): (60, 0),
+    ("w2", 1, 0): (0, 0), ("w2", 1, 1): (16, 0),
 }
 ADD = mybir.AluOpType.add
 

@@ -53,7 +53,6 @@ def tile_routed_moe_kernel(tc, xT, w1, w3, w2, offs, out):
         psum_y = ctx.enter_context(tc.psum_pool(name="psum_y", bufs=2))
 
         offs_t = lists.tile([P, E * C // 16], U16, name="offs_t")
-        nc.sync.dma_start(offs_t[:], offs)
 
         x_rows = xT.rearrange("(p j) n -> p j n", j=4)
         x_raw = []
@@ -61,6 +60,8 @@ def tile_routed_moe_kernel(tc, xT, w1, w3, w2, offs, out):
             t = keep.tile([P, 2, T], F32, name="x_raw%d" % u)
             nc.sync.dma_start(t[:], x_rows[:, 2 * u:2 * u + 2, :])
             x_raw.append(t)
+            if u == 0:
+                nc.sync.dma_start(offs_t[:], offs)
 
         steps = []
         for e in range(E):

from contextlib import ExitStack

import concourse.mybir as mybir

K, T, E, C, H, N = 512, 1024, 2, 256, 1024, 256
P = 128
FLOPS = 2 * E * C * (2 * K * H + H * N)

F32 = mybir.dt.float32
BF16 = mybir.dt.bfloat16
U32 = mybir.dt.uint32
U16 = mybir.dt.uint16
U8 = mybir.dt.uint8
FP8X4 = mybir.dt.float8_e4m3fn_x4
SILU = mybir.ActivationFunctionType.Silu
MULT = mybir.AluOpType.mult

CV_X = (168, 0)
SHARE = {
    ("w1", 0, 0): (44, 12), ("w3", 0, 0): (44, 12), ("w1", 0, 1): (44, 12), ("w3", 0, 1): (44, 12),
    ("w2", 0, 0): (24, 0), ("w2", 0, 1): (64, 0),
    ("w1", 1, 0): (44, 12), ("w3", 1, 0): (44, 12), ("w1", 1, 1): (44, 12), ("w3", 1, 1): (60, 0),
    ("w2", 1, 0): (0, 0), ("w2", 1, 1): (16, 0),
}
ADD = mybir.AluOpType.add


def split_copy(nc, dst, src, share, scalar_dst=None, scalar_src=None):
    scalar_dst = dst if scalar_dst is None else scalar_dst
    scalar_src = src if scalar_src is None else scalar_src
    n = dst.shape[1]
    a = share[0]
    b = share[0] + share[1]
    if a > 0:
        nc.vector.tensor_copy(out=dst[:, :a], in_=src[:, :a])
    if b > a:
        nc.gpsimd.tensor_scalar(out=dst[:, a:b], in0=src[:, a:b], scalar1=1.0, scalar2=0.0, op0=MULT, op1=ADD)
    if b < n:
        nc.scalar.copy(out=scalar_dst[:, b:], in_=scalar_src[:, b:])


def tile_routed_moe_kernel(tc, xT, w1, w3, w2, offs, out):
    nc = tc.nc
    with ExitStack() as ctx:
        lists = ctx.enter_context(tc.tile_pool(name="lists", bufs=1))
        keep = ctx.enter_context(tc.tile_pool(name="keep", bufs=1))
        grp_pool = ctx.enter_context(tc.tile_pool(name="grp_pool", bufs=4))
        sa_pool = ctx.enter_context(tc.tile_pool(name="sa_pool", bufs=3))
        hg_pool = ctx.enter_context(tc.tile_pool(name="hg_pool", bufs=2))
        y_pool = ctx.enter_context(tc.tile_pool(name="y_pool", bufs=4))
        psum_a = ctx.enter_context(tc.psum_pool(name="psum_a", bufs=3))
        psum_b = ctx.enter_context(tc.psum_pool(name="psum_b", bufs=3))
        psum_y = ctx.enter_context(tc.psum_pool(name="psum_y", bufs=2))

        offs_t = lists.tile([P, E * C // 16], U16, name="offs_t")

        x_rows = xT.rearrange("(p j) n -> p j n", j=4)
        x_raw = []
        for u in range(2):
            t = keep.tile([P, 2, T], F32, name="x_raw%d" % u)
            nc.sync.dma_start(t[:], x_rows[:, 2 * u:2 * u + 2, :])
            x_raw.append(t)
            if u == 0:
                nc.sync.dma_start(offs_t[:], offs)

        steps = []
        for e in range(E):
            for g in range(2):
                steps.append(("w1", e, g))
                steps.append(("w3", e, g))
        for e in range(E):
            for g in range(2):
                steps.append(("w2", e, g))

        raw = {}
        for st in steps:
            kind, e, g = st
            if kind == "w2":
                t = keep.tile([P, 4, N], F32, name="raw_%s_%d_%d" % st)
                nc.sync.dma_start(t[:], w2[e, 512 * g:512 * (g + 1), :].rearrange("(p j) n -> p j n", j=4))
            else:
                w = w1 if kind == "w1" else w3
                t = keep.tile([P, 4, 512], F32, name="raw_%s_%d_%d" % st)
                nc.sync.dma_start(t[:], w[e].rearrange("(p j) c -> p j c", j=4)[:, :, 512 * g:512 * (g + 1)])
            raw[st] = t

        win = []
        for nt in range(2):
            t = keep.tile([P, T], F32, name="win%d" % nt)
            nc.vector.memset(t[:], 0.0)
            win.append(t)
        warm_in = keep.tile([P, 1], F32, name="warm_in")
        warm_out = keep.tile([P, 1], F32, name="warm_out")
        nc.vector.memset(warm_in[:], 0.0)
        nc.scalar.activation(out=warm_out[:], in_=warm_in[:], func=SILU)

        xg = keep.tile([P, 4 * E * C], BF16, name="xg", align_bytes=64)
        xg_words = xg[:].bitcast(U32).rearrange("p (n u) -> p n u", u=2)
        for u in range(2):
            pair = keep.tile([P, 2 * T], BF16, name="pair%d" % u, align_bytes=64)
            split_copy(
                nc,
                pair[:].rearrange("p (c i e) -> p c e i", i=4, e=2),
                x_raw[u][:].rearrange("p e (c i) -> p c e i", i=4),
                CV_X,
            )
            nc.vector.tensor_copy(out=xg_words[:, :, u], in_=pair[:].bitcast(U32).indirect(offs_t[:]))
        xc = keep.tile([P, E * C], U32, name="xc", align_bytes=64)
        xs = keep.tile([P, E * C], U8, name="xs", align_bytes=64)

        grouped = {}
        codes = {}
        scales = {}
        sa = {}
        hg = {}
        hcodes = {}
        hscales = {}
        ybank = {}

        def cast(st):
            kind, e, g = st
            if kind == "w2":
                t = grp_pool.tile([P, 4 * N], BF16, name="grp2", tag="grp2", align_bytes=64)
                split_copy(
                    nc,
                    t[:].rearrange("p (c i j) -> p c j i", i=4, j=4),
                    raw[st][:].rearrange("p j (c i) -> p c j i", i=4),
                    SHARE[st],
                )
            else:
                t = grp_pool.tile([P, 4 * 512], BF16, name="grp", tag="grp", align_bytes=64)
                split_copy(
                    nc,
                    t[:].rearrange("p (t m j) -> p m j t", t=4, j=4),
                    raw[st][:].rearrange("p j (m t) -> p m j t", t=4),
                    SHARE[st],
                    t[:].rearrange("p (t m a b) -> p m a t b", t=4, a=2, b=2),
                    raw[st][:].rearrange("p (a b) (m t) -> p m a t b", b=2, t=4),
                )
            grouped[st] = t

        def quant(st):
            width = grouped[st].shape[1] // 4
            c = keep.tile([P, width], U32, name="c_%s_%d_%d" % st, align_bytes=64)
            s = keep.tile([P, width], U8, name="s_%s_%d_%d" % st, align_bytes=64)
            nc.vector.quantize_mx(out=c[:].bitcast(FP8X4), scales=s[:], in_=grouped[st][:])
            codes[st] = c
            scales[st] = s

        def stage1(st, pool, half):
            kind, e, g = st
            bank = pool.tile([P, 4, 128], F32, name="bank_" + kind, tag="bank_" + kind)
            cols = slice(e * C + 128 * half, e * C + 128 * (half + 1))
            for t in range(4):
                nc.tensor.matmul_mx(
                    out=bank[:, t, :],
                    lhsT=codes[st][:, 128 * t:128 * (t + 1)].bitcast(FP8X4),
                    lhsT_scale=scales[st][:, 128 * t:128 * (t + 1)],
                    rhs=xc[:, cols].bitcast(FP8X4),
                    rhs_scale=xs[:, cols],
                    start=True,
                    stop=True,
                )
            return bank

        def quant_h(e, g):
            c = keep.tile([P, C], U32, name="hc_%d_%d" % (e, g), align_bytes=64)
            s = keep.tile([P, C], U8, name="hs_%d_%d" % (e, g), align_bytes=64)
            nc.vector.quantize_mx(out=c[:].bitcast(FP8X4), scales=s[:], in_=hg[(e, g)][:])
            hcodes[(e, g)] = c
            hscales[(e, g)] = s

        def post(st):
            kind, e, g = st
            if kind == "w1":
                for half in range(2):
                    bank = stage1(st, psum_a, half)
                    t = sa_pool.tile([P, 512], F32, name="sa", tag="sa")
                    nc.scalar.activation(
                        out=t[:].rearrange("p (n t) -> p n t", t=4),
                        in_=bank[:].rearrange("p t n -> p n t"),
                        func=SILU,
                    )
                    sa[(e, g, half)] = t
            elif kind == "w3":
                h = hg_pool.tile([P, 4 * C], BF16, name="hg", tag="hg", align_bytes=64)
                hg[(e, g)] = h
                for half in range(2):
                    bank = stage1(st, psum_b, half)
                    nc.vector.tensor_tensor(
                        out=h[:, 512 * half:512 * (half + 1)].rearrange("p (n t) -> p n t", t=4),
                        in0=sa[(e, g, half)][:].rearrange("p (n t) -> p n t", t=4),
                        in1=bank[:].rearrange("p t n -> p n t"),
                        op=MULT,
                    )
                pending.append((e, g))

        def stage2():
            for e in range(E):
                for g in range(2):
                    if (e, g) in done2 or (e, g) not in hcodes or ("w2", e, g) not in codes:
                        continue
                    if g == 1 and (e, 0) not in done2:
                        continue
                    done2.add((e, g))
                    st = ("w2", e, g)
                    for nt in range(2):
                        if g == 0:
                            ybank[(e, nt)] = psum_y.tile([P, C], F32, name="ybank", tag="ybank")
                        nc.tensor.matmul_mx(
                            out=ybank[(e, nt)][:],
                            lhsT=codes[st][:, 128 * nt:128 * (nt + 1)].bitcast(FP8X4),
                            lhsT_scale=scales[st][:, 128 * nt:128 * (nt + 1)],
                            rhs=hcodes[(e, g)][:].bitcast(FP8X4),
                            rhs_scale=hscales[(e, g)][:],
                            start=(g == 0),
                            stop=(g == 1),
                        )
                    if g == 1:
                        for nt in range(2):
                            y = y_pool.tile([P, C], F32, name="y", tag="y")
                            nc.scalar.copy(out=y[:], in_=ybank[(e, nt)][:])
                            nc.vector.tensor_copy(
                                out=win[nt][:].indirect(offs_t[:, 16 * e:16 * (e + 1)]),
                                in_=y[:],
                            )
                            if e == E - 1:
                                nc.sync.dma_start(out[128 * nt:128 * (nt + 1), :], win[nt][:])

        done2 = set()
        pending = []
        cast(steps[0])
        nc.vector.quantize_mx(out=xc[:].bitcast(FP8X4), scales=xs[:], in_=xg[:])
        for i in range(len(steps)):
            if i + 1 < len(steps):
                cast(steps[i + 1])
            quant(steps[i])
            for eg in pending:
                quant_h(eg[0], eg[1])
            pending.clear()
            stage2()
            post(steps[i])
        for eg in pending:
            quant_h(eg[0], eg[1])
        stage2()
